import numpy as np, ml_dtypes
CORES = [15,47,79,175,207]
N = 5
QP = 64
def setup_inputs(rng):
    m = 150 * rng.standard_normal((1, QP, 1), dtype=np.float32) + 3 * rng.standard_normal((N, QP, 1), dtype=np.float32)
    m = (m + rng.uniform(100, 300, (1, QP, 1)) * (rng.random((1, QP, 1)) < 0.7) * (rng.random((N, QP, 1)) < 0.5)).astype(np.float32)
    l = 20 * (1 + np.abs(rng.standard_normal((N, QP, 1), dtype=np.float32)))
    return {"o": (l * rng.standard_normal((N, QP, 128), dtype=np.float32) / 4).astype(ml_dtypes.bfloat16), "ml": np.concatenate([m, l], axis=2)}
def setup_inputs_big(rng):
    d = setup_inputs(rng)
    for k in ("o",): d[k] = (d[k].astype(np.float32) * 1048576.0).astype(d[k].dtype)
    return d
def setup_inputs_small(rng):
    d = setup_inputs(rng)
    for k in ("o",): d[k] = (d[k].astype(np.float32) * (1 / 1048576.0)).astype(d[k].dtype)
    return d
def setup_inputs_apart(rng):
    d = setup_inputs(rng)
    f = (10.0 ** rng.permutation(np.linspace(-1.5, 1.5, N))).astype(np.float32).reshape(N, 1, 1)
    for k in ("o",): d[k] = (d[k].astype(np.float32) * f).astype(d[k].dtype)
    return d
def reference(o, ml):
    O, ML = o.astype(np.float64), ml.astype(np.float64)
    m, l = ML[:, :, 0:1], ML[:, :, 1:2]
    f = np.exp(m - m.max(axis=0))
    y = ((f * O).sum(axis=0) / (f * l).sum(axis=0)).astype(ml_dtypes.bfloat16)
    return {"y": np.broadcast_to(y, (N,) + y.shape)}

@@ -1,0 +1,119 @@
+from concourse.bass import DstId, RemoteDMATransfer
+from concourse.mybir import AluOpType, AxisListType, ActivationFunctionType
+
+N = 5
+OC = 64
+ROW = OC + 3
+PW = OC + 2
+PITCH = 72
+ENGINES = 8
+NSQ = 16.0
+
+SCRATCH = {
+    "land": ("sbuf", [128, N * PITCH], "bfloat16"),
+    "prod": ("sbuf", [128, N * PITCH], "bfloat16"),
+    "mlb": ("sbuf", [128, 2], "float32"),
+    "ident": ("sbuf", [128, 128], "bfloat16"),
+    "s": ("sbuf", [128, N], "float32"),
+    "negr": ("sbuf", [128, 1], "float32"),
+    "w": ("sbuf", [128, N], "float32"),
+    "f": ("sbuf", [128, N], "float32"),
+    "rden": ("sbuf", [128, 1], "float32"),
+    "yb": ("sbuf", [128, OC], "bfloat16"),
+    "acc": ("psum", [128, 128], "float32"),
+}
+SEMAPHORES = ["ld_ml", "ld_o", "ones", "idn", "split", "arrived", "sent", "ab", "ch", "f16",
+              "p0", "p1", "p2", "p3", "p4", "mm", "rd", "yd", "st"]
+
+
+def rank_program(g, core, T, topo):
+    rank = T.rank_of(core)
+    if rank is None:
+        return
+    S = T.sem
+    v, a, pe, sy = g.vector, g.scalar, g.tensor, g.sync
+    land, prod = T.land, T.prod
+    peers = [c for c in T.cores if c != core]
+    own = rank * PITCH
+    Sq, Cp = ActivationFunctionType.Square, ActivationFunctionType.Copy
+
+    sy.dma_start(T.mlb[0:128:2, :], T.ml[:, :]).then_inc(S.ld_ml, 16)
+    a.dma_start(T.mlb[1:128:2, :], T.ml[:, :]).then_inc(S.ld_ml, 16)
+    sy.dma_start(land[:, own:own + OC], T.o[:, :]).then_inc(S.ld_o, 16)
+
+    v.memset(T.ident[:, :], 1.0).then_inc(S.ones, 1)
+    g.wait_ge(S.ones, 1)
+    g.affine_select(T.ident[:, :], T.ident[:, :], [[-1, 128]], AluOpType.is_equal, 0.0, 0, 1).then_inc(S.idn, 1)
+
+    v.wait_ge(S.ld_ml, 32)
+    v.tensor_copy(land[:, own + OC:own + OC + 2], T.mlb[:, 0:2]).then_inc(S.split, 1)
+    v.wait_ge(S.split, 1)
+    v.tensor_tensor(land[:, own + OC + 2:own + ROW], T.mlb[:, 0:1], land[:, own + OC:own + OC + 1],
+                    AluOpType.subtract).then_inc(S.split, 1)
+
+    allowed = topo.mask(core, peers[0])
+    for d in peers:
+        allowed &= topo.mask(core, d)
+    engines = [e for e in range(16) if (allowed >> e) & 1][:ENGINES]
+    mask = 0
+    for e in engines:
+        mask |= 1 << e
+    ids = []
+    for d in peers:
+        rid, pid = topo.addr(d, core)
+        ids.append(DstId(rid=rid, pnc=pid))
+    piece = land[:, own:own + ROW]
+    g.wait_ge(S.ld_o, 16)
+    g.wait_ge(S.split, 2)
+    g.remote_dma_fused([RemoteDMATransfer(dst_ids=ids, dma_engine_mask=mask, remote_sem=S.arrived,
+                                          srcs=[piece], dsts=[piece for _ in peers], alu_op=0)], local_sem=S.sent)
+
+    got = len(engines) * len(peers)
+    hi = land[:, OC:N * PITCH:PITCH]
+    lo = land[:, OC + 2:N * PITCH:PITCH]
+    v.wait_ge(S.arrived, got)
+    v.wait_ge(S.split, 2)
+    v.tensor_tensor(T.s[:, :], hi, lo, AluOpType.add).then_inc(S.ab, 1)
+    v.tensor_reduce(T.negr[:, :], hi, AxisListType.X, AluOpType.max, negate=True).then_inc(S.ab, 1)
+    v.wait_ge(S.ab, 2)
+    v.tensor_scalar(T.w[:, :], T.s[:, :], T.negr[:, 0:1], -NSQ, AluOpType.add, AluOpType.max).then_inc(S.ch, 1)
+    a.wait_ge(S.ch, 1)
+    a.activation(T.w[:, :], T.w[:, :], Sq, bias=1.0, scale=1.0 / NSQ).then_inc(S.ch, 1)
+    a.wait_ge(S.ch, 2)
+    a.activation(T.w[:, :], T.w[:, :], Sq, bias=1.0).then_inc(S.ch, 1)
+    a.wait_ge(S.ch, 3)
+    a.activation(T.w[:, :], T.w[:, :], Sq).then_inc(S.ch, 1)
+    a.wait_ge(S.ch, 4)
+    a.activation(T.w[:, :], T.w[:, :], Sq).then_inc(S.ch, 1)
+    a.wait_ge(S.ch, 5)
+    a.activation(T.f[:, :], T.w[:, :], Sq).then_inc(S.f16, 1)
+
+    v.wait_ge(S.ch, 5)
+    v.wait_ge(S.ld_o, 16)
+    for j in (0, 1, 2):
+        c = j * PITCH
+        v.tensor_scalar(prod[:, c:c + PW], land[:, c:c + PW], T.w[:, j:j + 1], T.w[:, j:j + 1],
+                        AluOpType.mult, AluOpType.mult).then_inc(S["p%d" % j], 1)
+    a.wait_ge(S.f16, 1)
+    a.wait_ge(S.arrived, got)
+    a.wait_ge(S.ld_o, 16)
+    a.wait_ge(S.split, 2)
+    for j in (3, 4):
+        c = j * PITCH
+        a.activation(prod[:, c:c + PW], land[:, c:c + PW], Cp, scale=T.f[:, j:j + 1]).then_inc(S["p%d" % j], 1)
+
+    pe.wait_ge(S.idn, 1)
+    order = (0, 1, 3, 2, 4)
+    for k, j in enumerate(order):
+        c = j * PITCH
+        pe.wait_ge(S["p%d" % j], 1)
+        pe.matmul(T.acc[:, 0:PW], T.ident[:, :], prod[:, c:c + PW], k == 0, k == N - 1).then_inc(S.mm, 1)
+
+    v.wait_ge(S.mm, N)
+    v.reciprocal(T.rden[:, :], T.acc[:, PW - 1:PW]).then_inc(S.rd, 1)
+    v.wait_ge(S.rd, 1)
+    v.tensor_scalar(T.yb[:, :], T.acc[:, 0:OC], T.rden[:, 0:1], None, AluOpType.mult).then_inc(S.yd, 1)
+    sy.wait_ge(S.yd, 1)
+    sy.dma_start(T.y[:, :], T.yb[:, :]).then_inc(S.st, 16)
+    sy.wait_ge(S.st, 16)
+    g.wait_ge(S.sent, len(engines))

@@ -3,27 +3,31 @@ from concourse.mybir import AluOpType, AxisListType, ActivationFunctionType
 
 N = 5
 OC = 64
-ROW = OC + 3
-PW = OC + 2
+CL, CH, CN = OC, OC + 2, OC + 3
+ROW = OC + 4
 PITCH = 72
 ENGINES = 8
-NSQ = 16.0
+A_FIT, C_FIT = 0.1075, 0.73
+K = 100663296.0
 
 SCRATCH = {
     "land": ("sbuf", [128, N * PITCH], "bfloat16"),
     "prod": ("sbuf", [128, N * PITCH], "bfloat16"),
-    "mlb": ("sbuf", [128, 2], "float32"),
+    "d0": ("sbuf", [128, 4], "float32"),
+    "d1": ("sbuf", [128, 8], "float32"),
     "ident": ("sbuf", [128, 128], "bfloat16"),
     "s": ("sbuf", [128, N], "float32"),
     "negr": ("sbuf", [128, 1], "float32"),
     "w": ("sbuf", [128, N], "float32"),
     "f": ("sbuf", [128, N], "float32"),
+    "fl": ("sbuf", [128, N], "float32"),
+    "den": ("sbuf", [128, 1], "float32"),
     "rden": ("sbuf", [128, 1], "float32"),
     "yb": ("sbuf", [128, OC], "bfloat16"),
     "acc": ("psum", [128, 128], "float32"),
 }
-SEMAPHORES = ["ld_ml", "ld_o", "ones", "idn", "split", "arrived", "sent", "ab", "ch", "f16",
-              "p0", "p1", "p2", "p3", "p4", "mm", "rd", "yd", "st"]
+SEMAPHORES = ["ld_ml", "ld_o", "ones", "idn", "cst", "split", "arrived", "sent", "ab",
+              "ch", "fin", "p0", "p1", "p2", "p3", "p4", "mm", "fld", "dn", "rd", "yd", "st"]
 
 
 def rank_program(g, core, T, topo):
@@ -33,23 +37,28 @@ def rank_program(g, core, T, topo):
     S = T.sem
     v, a, pe, sy = g.vector, g.scalar, g.tensor, g.sync
     land, prod = T.land, T.prod
-    peers = [c for c in T.cores if c != core]
+    peers = [T.cores[(rank + k) % N] for k in range(1, N)]
     own = rank * PITCH
     Sq, Cp = ActivationFunctionType.Square, ActivationFunctionType.Copy
 
-    sy.dma_start(T.mlb[0:128:2, :], T.ml[:, :]).then_inc(S.ld_ml, 16)
-    a.dma_start(T.mlb[1:128:2, :], T.ml[:, :]).then_inc(S.ld_ml, 16)
+    sy.dma_start(T.d1[0:128:2, 4:6], T.ml[:, :]).then_inc(S.ld_ml, 16)
+    a.dma_start(T.d1[1:128:2, 4:6], T.ml[:, :]).then_inc(S.ld_ml, 16)
     sy.dma_start(land[:, own:own + OC], T.o[:, :]).then_inc(S.ld_o, 16)
 
     v.memset(T.ident[:, :], 1.0).then_inc(S.ones, 1)
     g.wait_ge(S.ones, 1)
     g.affine_select(T.ident[:, :], T.ident[:, :], [[-1, 128]], AluOpType.is_equal, 0.0, 0, 1).then_inc(S.idn, 1)
+    v.memset(T.d0[:, 0:1], K).then_inc(S.cst, 1)
+    v.memset(T.d0[:, 1:2], -K).then_inc(S.cst, 1)
+    v.memset(T.d0[:, 2:3], 0.0).then_inc(S.cst, 1)
+    v.memset(T.d1[:, 0:4], 0.0).then_inc(S.cst, 1)
 
+    v.wait_ge(S.cst, 4)
     v.wait_ge(S.ld_ml, 32)
-    v.tensor_copy(land[:, own + OC:own + OC + 2], T.mlb[:, 0:2]).then_inc(S.split, 1)
-    v.wait_ge(S.split, 1)
-    v.tensor_tensor(land[:, own + OC + 2:own + ROW], T.mlb[:, 0:1], land[:, own + OC:own + OC + 1],
-                    AluOpType.subtract).then_inc(S.split, 1)
+    v.tensor_tensor_scan(land[:, own + OC + 1:own + ROW], T.d0[:, 0:3], T.d1[:, 2:5], T.d1[:, 4:5],
+                         AluOpType.add, AluOpType.subtract).then_inc(S.split, 1)
+    a.wait_ge(S.ld_ml, 32)
+    a.activation(land[:, own + CL:own + CL + 1], T.d1[:, 5:6], Cp).then_inc(S.split, 1)
 
     allowed = topo.mask(core, peers[0])
     for d in peers:
@@ -69,49 +78,48 @@ def rank_program(g, core, T, topo):
                                           srcs=[piece], dsts=[piece for _ in peers], alu_op=0)], local_sem=S.sent)
 
     got = len(engines) * len(peers)
-    hi = land[:, OC:N * PITCH:PITCH]
-    lo = land[:, OC + 2:N * PITCH:PITCH]
     v.wait_ge(S.arrived, got)
     v.wait_ge(S.split, 2)
-    v.tensor_tensor(T.s[:, :], hi, lo, AluOpType.add).then_inc(S.ab, 1)
-    v.tensor_reduce(T.negr[:, :], hi, AxisListType.X, AluOpType.max, negate=True).then_inc(S.ab, 1)
+    v.tensor_tensor(T.s[:, :], land[:, CH:N * PITCH:PITCH], land[:, CN:N * PITCH:PITCH],
+                    AluOpType.subtract).then_inc(S.ab, 1)
+    v.wait_ge(S.ab, 1)
+    v.tensor_reduce(T.negr[:, :], T.s[:, :], AxisListType.X, AluOpType.max, negate=True).then_inc(S.ab, 1)
     v.wait_ge(S.ab, 2)
-    v.tensor_scalar(T.w[:, :], T.s[:, :], T.negr[:, 0:1], -NSQ, AluOpType.add, AluOpType.max).then_inc(S.ch, 1)
+    v.tensor_scalar(T.w[:, :], T.s[:, :], T.negr[:, 0:1], -1.0 / A_FIT, AluOpType.add, AluOpType.max).then_inc(S.ch, 1)
     a.wait_ge(S.ch, 1)
-    a.activation(T.w[:, :], T.w[:, :], Sq, bias=1.0, scale=1.0 / NSQ).then_inc(S.ch, 1)
+    a.activation(T.w[:, :], T.w[:, :], Sq, bias=1.0, scale=A_FIT).then_inc(S.ch, 1)
     a.wait_ge(S.ch, 2)
-    a.activation(T.w[:, :], T.w[:, :], Sq, bias=1.0).then_inc(S.ch, 1)
+    a.activation(T.w[:, :], T.w[:, :], Sq, bias=C_FIT).then_inc(S.ch, 1)
     a.wait_ge(S.ch, 3)
     a.activation(T.w[:, :], T.w[:, :], Sq).then_inc(S.ch, 1)
     a.wait_ge(S.ch, 4)
-    a.activation(T.w[:, :], T.w[:, :], Sq).then_inc(S.ch, 1)
-    a.wait_ge(S.ch, 5)
-    a.activation(T.f[:, :], T.w[:, :], Sq).then_inc(S.f16, 1)
+    a.activation(T.f[:, :], T.w[:, :], Sq).then_inc(S.fin, 1)
 
-    v.wait_ge(S.ch, 5)
+    v.wait_ge(S.ch, 4)
     v.wait_ge(S.ld_o, 16)
-    for j in (0, 1, 2):
-        c = j * PITCH
-        v.tensor_scalar(prod[:, c:c + PW], land[:, c:c + PW], T.w[:, j:j + 1], T.w[:, j:j + 1],
-                        AluOpType.mult, AluOpType.mult).then_inc(S["p%d" % j], 1)
-    a.wait_ge(S.f16, 1)
+    v.tensor_scalar(prod[:, 0:OC], land[:, 0:OC], T.w[:, 0:1], T.w[:, 0:1],
+                    AluOpType.mult, AluOpType.mult).then_inc(S.p0, 1)
+    a.wait_ge(S.fin, 1)
     a.wait_ge(S.arrived, got)
     a.wait_ge(S.ld_o, 16)
-    a.wait_ge(S.split, 2)
-    for j in (3, 4):
+    for j in range(1, N):
         c = j * PITCH
-        a.activation(prod[:, c:c + PW], land[:, c:c + PW], Cp, scale=T.f[:, j:j + 1]).then_inc(S["p%d" % j], 1)
-
+        a.activation(prod[:, c:c + OC], land[:, c:c + OC], Cp, scale=T.f[:, j:j + 1]).then_inc(S["p%d" % j], 1)
     pe.wait_ge(S.idn, 1)
-    order = (0, 1, 3, 2, 4)
-    for k, j in enumerate(order):
+    for j in range(N):
         c = j * PITCH
         pe.wait_ge(S["p%d" % j], 1)
-        pe.matmul(T.acc[:, 0:PW], T.ident[:, :], prod[:, c:c + PW], k == 0, k == N - 1).then_inc(S.mm, 1)
+        pe.matmul(T.acc[:, 0:OC], T.ident[:, :], prod[:, c:c + OC], j == 0, j == N - 1).then_inc(S.mm, 1)
 
-    v.wait_ge(S.mm, N)
-    v.reciprocal(T.rden[:, :], T.acc[:, PW - 1:PW]).then_inc(S.rd, 1)
+    v.wait_ge(S.fin, 1)
+    v.tensor_tensor(T.fl[:, :], T.f[:, :], land[:, CL:N * PITCH:PITCH], AluOpType.mult).then_inc(S.fld, 1)
+    v.wait_ge(S.fld, 1)
+    v.tensor_reduce(T.den[:, :], T.fl[:, :], AxisListType.X, AluOpType.add).then_inc(S.dn, 1)
+    v.wait_ge(S.dn, 1)
+    v.reciprocal(T.rden[:, :], T.den[:, :]).then_inc(S.rd, 1)
+
     v.wait_ge(S.rd, 1)
+    v.wait_ge(S.mm, N)
     v.tensor_scalar(T.yb[:, :], T.acc[:, 0:OC], T.rden[:, 0:1], None, AluOpType.mult).then_inc(S.yd, 1)
     sy.wait_ge(S.yd, 1)
     sy.dma_start(T.y[:, :], T.yb[:, :]).then_inc(S.st, 16)

@@ -2,32 +2,36 @@ from concourse.bass import DstId, RemoteDMATransfer
 from concourse.mybir import AluOpType, AxisListType, ActivationFunctionType
 
 N = 5
-OC = 64
-CL, CH, CN = OC, OC + 2, OC + 3
-ROW = OC + 4
-PITCH = 72
-ENGINES = 8
-A_FIT, C_FIT = 0.1075, 0.73
-K = 100663296.0
+Q = 64
+D = 128
 
 SCRATCH = {
-    "land": ("sbuf", [128, N * PITCH], "bfloat16"),
-    "prod": ("sbuf", [128, N * PITCH], "bfloat16"),
-    "d0": ("sbuf", [128, 4], "float32"),
-    "d1": ("sbuf", [128, 8], "float32"),
-    "ident": ("sbuf", [128, 128], "bfloat16"),
-    "s": ("sbuf", [128, N], "float32"),
-    "negr": ("sbuf", [128, 1], "float32"),
-    "w": ("sbuf", [128, N], "float32"),
+    "oD": ("dram", [N, 128, Q], "bfloat16"),
+    "mD": ("dram", [N + 1, 128, 1], "float32"),
+    "oA": ("sbuf", [128, D], "bfloat16"),
+    "oB": ("sbuf", [128, D], "bfloat16"),
+    "oC": ("sbuf", [128, D], "bfloat16"),
+    "mT": ("sbuf", [128, 256], "float32"),
+    "zb": ("sbuf", [128, Q], "bfloat16"),
+    "ob": ("sbuf", [128, Q], "bfloat16"),
+    "sel": ("sbuf", [128, Q], "bfloat16"),
+    "of": ("sbuf", [128, 8], "float32"),
+    "i5": ("sbuf", [128, 8], "float32"),
+    "negM": ("sbuf", [128, 1], "float32"),
     "f": ("sbuf", [128, N], "float32"),
     "fl": ("sbuf", [128, N], "float32"),
     "den": ("sbuf", [128, 1], "float32"),
     "rden": ("sbuf", [128, 1], "float32"),
-    "yb": ("sbuf", [128, OC], "bfloat16"),
-    "acc": ("psum", [128, 128], "float32"),
+    "wA": ("sbuf", [128, Q], "bfloat16"),
+    "wB": ("sbuf", [128, Q], "bfloat16"),
+    "wC": ("sbuf", [128, Q], "bfloat16"),
+    "yb": ("sbuf", [128, D], "bfloat16"),
+    "psM": ("psum", [128, 512], "float32"),
+    "psL": ("psum", [128, 512], "float32"),
+    "acc": ("psum", [128, 512], "float32"),
 }
-SEMAPHORES = ["ld_ml", "ld_o", "ones", "idn", "cst", "split", "arrived", "sent", "ab",
-              "ch", "fin", "p0", "p1", "p2", "p3", "p4", "mm", "fld", "dn", "rd", "yd", "st"]
+SEMAPHORES = ["ld_m", "ld_m2", "ld_o", "ld_a", "cz", "cf", "ones", "idn5", "seld", "arr_m", "arr_o", "sent", "mt",
+              "pm", "pl", "ng", "fd", "fld", "dn", "rd", "wa", "wb", "wc", "tb", "tc", "mm", "yd", "st"]
 
 
 def rank_program(g, core, T, topo):
@@ -36,92 +40,98 @@ def rank_program(g, core, T, topo):
         return
     S = T.sem
     v, a, pe, sy = g.vector, g.scalar, g.tensor, g.sync
-    land, prod = T.land, T.prod
-    peers = [T.cores[(rank + k) % N] for k in range(1, N)]
-    own = rank * PITCH
-    Sq, Cp = ActivationFunctionType.Square, ActivationFunctionType.Copy
+    Ex, Cp = ActivationFunctionType.Exp, ActivationFunctionType.Copy
+    steps = list(range(1, N))
+    peers = [T.cores[(rank + k) % N] for k in steps]
+    slots = [N - k for k in steps]
 
-    sy.dma_start(T.d1[0:128:2, 4:6], T.ml[:, :]).then_inc(S.ld_ml, 16)
-    a.dma_start(T.d1[1:128:2, 4:6], T.ml[:, :]).then_inc(S.ld_ml, 16)
-    sy.dma_start(land[:, own:own + OC], T.o[:, :]).then_inc(S.ld_o, 16)
+    a.dma_start(T.mD[0], T.ml[:, :]).then_inc(S.ld_m, 16)
+    sy.dma_start(T.oD[0], T.o[:, :]).then_inc(S.ld_o, 16)
+    a.dma_start(T.mD[N], T.ml[:, :]).then_inc(S.ld_m2, 16)
+    sy.dma_start(T.oA[0:Q, :], T.o[:, :]).then_inc(S.ld_a, 16)
 
-    v.memset(T.ident[:, :], 1.0).then_inc(S.ones, 1)
-    g.wait_ge(S.ones, 1)
-    g.affine_select(T.ident[:, :], T.ident[:, :], [[-1, 128]], AluOpType.is_equal, 0.0, 0, 1).then_inc(S.idn, 1)
-    v.memset(T.d0[:, 0:1], K).then_inc(S.cst, 1)
-    v.memset(T.d0[:, 1:2], -K).then_inc(S.cst, 1)
-    v.memset(T.d0[:, 2:3], 0.0).then_inc(S.cst, 1)
-    v.memset(T.d1[:, 0:4], 0.0).then_inc(S.cst, 1)
-
-    v.wait_ge(S.cst, 4)
-    v.wait_ge(S.ld_ml, 32)
-    v.tensor_tensor_scan(land[:, own + OC + 1:own + ROW], T.d0[:, 0:3], T.d1[:, 2:5], T.d1[:, 4:5],
-                         AluOpType.add, AluOpType.subtract).then_inc(S.split, 1)
-    a.wait_ge(S.ld_ml, 32)
-    a.activation(land[:, own + CL:own + CL + 1], T.d1[:, 5:6], Cp).then_inc(S.split, 1)
+    v.memset(T.zb[:, :], 0.0).then_inc(S.cz, 1)
+    v.memset(T.of[0:N, 0:N], 1.0).then_inc(S.cf, 1)
+    a.wait_ge(S.cz, 1)
+    a.activation(T.ob[:, :], T.zb[:, :], Ex).then_inc(S.ones, 1)
 
     allowed = topo.mask(core, peers[0])
     for d in peers:
         allowed &= topo.mask(core, d)
-    engines = [e for e in range(16) if (allowed >> e) & 1][:ENGINES]
-    mask = 0
+    engines = [e for e in range(16) if (allowed >> e) & 1]
+    while 128 % len(engines):
+        engines.pop()
+    mask_o = 0
     for e in engines:
-        mask |= 1 << e
+        mask_o |= 1 << e
+    mask_m = 1 << engines[0]
     ids = []
     for d in peers:
         rid, pid = topo.addr(d, core)
         ids.append(DstId(rid=rid, pnc=pid))
-    piece = land[:, own:own + ROW]
+    g.wait_ge(S.ld_m, 16)
+    g.remote_dma_fused([RemoteDMATransfer(dst_ids=ids, dma_engine_mask=mask_m, remote_sem=S.arr_m,
+                                          srcs=[T.mD[0]], dsts=[T.mD[k] for k in slots], alu_op=0)], local_sem=S.sent)
     g.wait_ge(S.ld_o, 16)
-    g.wait_ge(S.split, 2)
-    g.remote_dma_fused([RemoteDMATransfer(dst_ids=ids, dma_engine_mask=mask, remote_sem=S.arrived,
-                                          srcs=[piece], dsts=[piece for _ in peers], alu_op=0)], local_sem=S.sent)
+    g.remote_dma_fused([RemoteDMATransfer(dst_ids=ids, dma_engine_mask=mask_o, remote_sem=S.arr_o,
+                                          srcs=[T.oD[0]], dsts=[T.oD[k] for k in slots], alu_op=0)], local_sem=S.sent)
+    got_m, got_o = len(peers), len(engines) * len(peers)
 
-    got = len(engines) * len(peers)
-    v.wait_ge(S.arrived, got)
-    v.wait_ge(S.split, 2)
-    v.tensor_tensor(T.s[:, :], land[:, CH:N * PITCH:PITCH], land[:, CN:N * PITCH:PITCH],
-                    AluOpType.subtract).then_inc(S.ab, 1)
-    v.wait_ge(S.ab, 1)
-    v.tensor_reduce(T.negr[:, :], T.s[:, :], AxisListType.X, AluOpType.max, negate=True).then_inc(S.ab, 1)
-    v.wait_ge(S.ab, 2)
-    v.tensor_scalar(T.w[:, :], T.s[:, :], T.negr[:, 0:1], -1.0 / A_FIT, AluOpType.add, AluOpType.max).then_inc(S.ch, 1)
-    a.wait_ge(S.ch, 1)
-    a.activation(T.w[:, :], T.w[:, :], Sq, bias=1.0, scale=A_FIT).then_inc(S.ch, 1)
-    a.wait_ge(S.ch, 2)
-    a.activation(T.w[:, :], T.w[:, :], Sq, bias=C_FIT).then_inc(S.ch, 1)
-    a.wait_ge(S.ch, 3)
-    a.activation(T.w[:, :], T.w[:, :], Sq).then_inc(S.ch, 1)
-    a.wait_ge(S.ch, 4)
-    a.activation(T.f[:, :], T.w[:, :], Sq).then_inc(S.fin, 1)
+    g.wait_ge(S.cf, 1)
+    g.affine_select(T.i5[0:N, 0:N], T.of[0:N, 0:N], [[-1, N]], AluOpType.is_equal, 0.0, 0, 1).then_inc(S.idn5, 1)
+    g.wait_ge(S.ones, 1)
+    g.affine_select(T.sel[0:Q, :], T.ob[0:Q, :], [[-1, Q]], AluOpType.is_equal, 0.0, 0, 1).then_inc(S.seld, 1)
+    g.affine_select(T.sel[Q:128, :], T.ob[Q:128, :], [[-1, Q]], AluOpType.is_equal, 0.0, 0, 1).then_inc(S.seld, 1)
 
-    v.wait_ge(S.ch, 4)
-    v.wait_ge(S.ld_o, 16)
-    v.tensor_scalar(prod[:, 0:OC], land[:, 0:OC], T.w[:, 0:1], T.w[:, 0:1],
-                    AluOpType.mult, AluOpType.mult).then_inc(S.p0, 1)
-    a.wait_ge(S.fin, 1)
-    a.wait_ge(S.arrived, got)
-    a.wait_ge(S.ld_o, 16)
-    for j in range(1, N):
-        c = j * PITCH
-        a.activation(prod[:, c:c + OC], land[:, c:c + OC], Cp, scale=T.f[:, j:j + 1]).then_inc(S["p%d" % j], 1)
-    pe.wait_ge(S.idn, 1)
-    for j in range(N):
-        c = j * PITCH
-        pe.wait_ge(S["p%d" % j], 1)
-        pe.matmul(T.acc[:, 0:OC], T.ident[:, :], prod[:, c:c + OC], j == 0, j == N - 1).then_inc(S.mm, 1)
+    sy.wait_ge(S.arr_m, got_m)
+    sy.wait_ge(S.ld_m, 16)
+    sy.dma_start(T.mT[0:N, 0:128], T.mD[0:N]).then_inc(S.mt, 16)
+    a.wait_ge(S.arr_m, got_m)
+    a.wait_ge(S.ld_m2, 16)
+    a.dma_start(T.mT[0:N, 128:256], T.mD[1:N + 1]).then_inc(S.mt, 16)
 
-    v.wait_ge(S.fin, 1)
-    v.tensor_tensor(T.fl[:, :], T.f[:, :], land[:, CL:N * PITCH:PITCH], AluOpType.mult).then_inc(S.fld, 1)
+    sy.wait_ge(S.arr_o, got_o)
+    sy.dma_start(T.oB[:, :], T.oD[1:3]).then_inc(S.tb, 16)
+    sy.dma_start(T.oC[:, :], T.oD[3:5]).then_inc(S.tc, 16)
+
+    pe.wait_ge(S.mt, 32)
+    pe.wait_ge(S.idn5, 1)
+    pe.matmul(T.psM[:, 0:N], T.mT[0:N, 0:256:2], T.i5[0:N, 0:N], True, True).then_inc(S.pm, 1)
+    pe.matmul(T.psL[:, 0:N], T.mT[0:N, 1:256:2], T.i5[0:N, 0:N], True, True).then_inc(S.pl, 1)
+
+    v.wait_ge(S.pm, 1)
+    v.tensor_reduce(T.negM[:, :], T.psM[:, 0:N], AxisListType.X, AluOpType.max, negate=True).then_inc(S.ng, 1)
+    a.wait_ge(S.pm, 1)
+    a.wait_ge(S.ng, 1)
+    a.activation(T.f[:, :], T.psM[:, 0:N], Ex, bias=T.negM[:, 0:1]).then_inc(S.fd, 1)
+
+    a.wait_ge(S.fd, 1)
+    a.wait_ge(S.seld, 2)
+    a.activation(T.wA[0:Q, :], T.sel[0:Q, :], Cp, scale=T.f[0:Q, 0:1]).then_inc(S.wa, 1)
+    a.activation(T.wB[:, :], T.sel[:, :], Cp, scale=T.f[:, 1:2]).then_inc(S.wb, 1)
+    a.activation(T.wC[:, :], T.sel[:, :], Cp, scale=T.f[:, 3:4]).then_inc(S.wc, 1)
+    v.wait_ge(S.fd, 1)
+    v.wait_ge(S.pl, 1)
+    v.tensor_tensor(T.fl[:, :], T.f[:, :], T.psL[:, 0:N], AluOpType.mult).then_inc(S.fld, 1)
     v.wait_ge(S.fld, 1)
     v.tensor_reduce(T.den[:, :], T.fl[:, :], AxisListType.X, AluOpType.add).then_inc(S.dn, 1)
     v.wait_ge(S.dn, 1)
     v.reciprocal(T.rden[:, :], T.den[:, :]).then_inc(S.rd, 1)
 
+    pe.wait_ge(S.wa, 1)
+    pe.wait_ge(S.ld_a, 16)
+    pe.matmul(T.acc[0:Q, 0:D], T.wA[0:Q, :], T.oA[0:Q, :], True, False).then_inc(S.mm, 1)
+    pe.wait_ge(S.wb, 1)
+    pe.wait_ge(S.tb, 16)
+    pe.matmul(T.acc[0:Q, 0:D], T.wB[:, :], T.oB[:, :], False, False).then_inc(S.mm, 1)
+    pe.wait_ge(S.wc, 1)
+    pe.wait_ge(S.tc, 16)
+    pe.matmul(T.acc[0:Q, 0:D], T.wC[:, :], T.oC[:, :], False, True).then_inc(S.mm, 1)
+
     v.wait_ge(S.rd, 1)
-    v.wait_ge(S.mm, N)
-    v.tensor_scalar(T.yb[:, :], T.acc[:, 0:OC], T.rden[:, 0:1], None, AluOpType.mult).then_inc(S.yd, 1)
+    v.wait_ge(S.mm, 3)
+    v.tensor_scalar(T.yb[0:Q, :], T.acc[0:Q, 0:D], T.rden[0:Q, 0:1], None, AluOpType.mult).then_inc(S.yd, 1)
     sy.wait_ge(S.yd, 1)
-    sy.dma_start(T.y[:, :], T.yb[:, :]).then_inc(S.st, 16)
+    sy.dma_start(T.y[:, :], T.yb[0:Q, :]).then_inc(S.st, 16)
     sy.wait_ge(S.st, 16)
-    g.wait_ge(S.sent, len(engines))
+    g.wait_ge(S.sent, 1 + len(engines))

@@ -4,6 +4,7 @@ from concourse.mybir import AluOpType, AxisListType, ActivationFunctionType
 N = 5
 Q = 64
 D = 128
+H = D // 2
 
 SCRATCH = {
     "oD": ("dram", [N, 128, Q], "bfloat16"),
@@ -12,26 +13,32 @@ SCRATCH = {
     "oB": ("sbuf", [128, D], "bfloat16"),
     "oC": ("sbuf", [128, D], "bfloat16"),
     "mT": ("sbuf", [128, 256], "float32"),
+    "mlS": ("sbuf", [128, 2], "float32"),
     "zb": ("sbuf", [128, Q], "bfloat16"),
     "ob": ("sbuf", [128, Q], "bfloat16"),
     "sel": ("sbuf", [128, Q], "bfloat16"),
     "of": ("sbuf", [128, 8], "float32"),
     "i5": ("sbuf", [128, 8], "float32"),
     "negM": ("sbuf", [128, 1], "float32"),
-    "f": ("sbuf", [128, N], "float32"),
-    "fl": ("sbuf", [128, N], "float32"),
-    "den": ("sbuf", [128, 1], "float32"),
+    "fb": ("sbuf", [128, 8], "bfloat16"),
+    "f3": ("sbuf", [128, 1], "float32"),
     "rden": ("sbuf", [128, 1], "float32"),
+    "lA": ("sbuf", [128, Q], "bfloat16"),
+    "lB": ("sbuf", [128, Q], "bfloat16"),
+    "lC": ("sbuf", [128, Q], "bfloat16"),
     "wA": ("sbuf", [128, Q], "bfloat16"),
     "wB": ("sbuf", [128, Q], "bfloat16"),
     "wC": ("sbuf", [128, Q], "bfloat16"),
     "yb": ("sbuf", [128, D], "bfloat16"),
     "psM": ("psum", [128, 512], "float32"),
     "psL": ("psum", [128, 512], "float32"),
-    "acc": ("psum", [128, 512], "float32"),
+    "psD": ("psum", [128, 512], "float32"),
+    "accL": ("psum", [128, 512], "float32"),
+    "accR": ("psum", [128, 512], "float32"),
 }
-SEMAPHORES = ["ld_m", "ld_m2", "ld_o", "ld_a", "cz", "cf", "ones", "idn5", "seld", "arr_m", "arr_o", "sent", "mt",
-              "pm", "pl", "ng", "fd", "fld", "dn", "rd", "wa", "wb", "wc", "tb", "tc", "mm", "yd", "st"]
+SEMAPHORES = ["ld_m", "ld_m2", "ld_o", "ld_a", "ld_s", "cz", "cf", "ones", "idn5", "seld", "arr_m", "arr_ob", "arr_oc", "sent",
+              "mt", "pm", "pl", "ng", "fd", "f3d", "la", "lb", "lc", "dd", "rd", "wa", "wb", "wc", "tb", "tc", "mml", "mmr",
+              "yd", "st"]
 
 
 def rank_program(g, core, T, topo):
@@ -41,6 +48,7 @@ def rank_program(g, core, T, topo):
     S = T.sem
     v, a, pe, sy = g.vector, g.scalar, g.tensor, g.sync
     Ex, Cp = ActivationFunctionType.Exp, ActivationFunctionType.Copy
+    mult = AluOpType.mult
     steps = list(range(1, N))
     peers = [T.cores[(rank + k) % N] for k in steps]
     slots = [N - k for k in steps]
@@ -49,6 +57,7 @@ def rank_program(g, core, T, topo):
     sy.dma_start(T.oD[0], T.o[:, :]).then_inc(S.ld_o, 16)
     a.dma_start(T.mD[N], T.ml[:, :]).then_inc(S.ld_m2, 16)
     sy.dma_start(T.oA[0:Q, :], T.o[:, :]).then_inc(S.ld_a, 16)
+    a.dma_start(T.mlS[0:Q, :], T.ml[:, :]).then_inc(S.ld_s, 16)
 
     v.memset(T.zb[:, :], 0.0).then_inc(S.cz, 1)
     v.memset(T.of[0:N, 0:N], 1.0).then_inc(S.cf, 1)
@@ -73,9 +82,11 @@ def rank_program(g, core, T, topo):
     g.remote_dma_fused([RemoteDMATransfer(dst_ids=ids, dma_engine_mask=mask_m, remote_sem=S.arr_m,
                                           srcs=[T.mD[0]], dsts=[T.mD[k] for k in slots], alu_op=0)], local_sem=S.sent)
     g.wait_ge(S.ld_o, 16)
-    g.remote_dma_fused([RemoteDMATransfer(dst_ids=ids, dma_engine_mask=mask_o, remote_sem=S.arr_o,
-                                          srcs=[T.oD[0]], dsts=[T.oD[k] for k in slots], alu_op=0)], local_sem=S.sent)
-    got_m, got_o = len(peers), len(engines) * len(peers)
+    g.remote_dma_fused([RemoteDMATransfer(dst_ids=ids[0:2], dma_engine_mask=mask_o, remote_sem=S.arr_oc,
+                                          srcs=[T.oD[0]], dsts=[T.oD[k] for k in slots[0:2]], alu_op=0)], local_sem=S.sent)
+    g.remote_dma_fused([RemoteDMATransfer(dst_ids=ids[2:4], dma_engine_mask=mask_o, remote_sem=S.arr_ob,
+                                          srcs=[T.oD[0]], dsts=[T.oD[k] for k in slots[2:4]], alu_op=0)], local_sem=S.sent)
+    got_m, got_pair = len(peers), 2 * len(engines)
 
     g.wait_ge(S.cf, 1)
     g.affine_select(T.i5[0:N, 0:N], T.of[0:N, 0:N], [[-1, N]], AluOpType.is_equal, 0.0, 0, 1).then_inc(S.idn5, 1)
@@ -90,48 +101,66 @@ def rank_program(g, core, T, topo):
     a.wait_ge(S.ld_m2, 16)
     a.dma_start(T.mT[0:N, 128:256], T.mD[1:N + 1]).then_inc(S.mt, 16)
 
-    sy.wait_ge(S.arr_o, got_o)
-    sy.dma_start(T.oB[:, :], T.oD[1:3]).then_inc(S.tb, 16)
+    sy.wait_ge(S.arr_oc, got_pair)
     sy.dma_start(T.oC[:, :], T.oD[3:5]).then_inc(S.tc, 16)
+    sy.wait_ge(S.arr_ob, got_pair)
+    sy.dma_start(T.oB[:, :], T.oD[1:3]).then_inc(S.tb, 16)
 
     pe.wait_ge(S.mt, 32)
     pe.wait_ge(S.idn5, 1)
     pe.matmul(T.psM[:, 0:N], T.mT[0:N, 0:256:2], T.i5[0:N, 0:N], True, True).then_inc(S.pm, 1)
     pe.matmul(T.psL[:, 0:N], T.mT[0:N, 1:256:2], T.i5[0:N, 0:N], True, True).then_inc(S.pl, 1)
 
+    v.wait_ge(S.seld, 2)
+    v.wait_ge(S.ld_s, 16)
+    v.tensor_scalar(T.lA[0:Q, :], T.sel[0:Q, :], T.mlS[0:Q, 1:2], None, mult).then_inc(S.la, 1)
     v.wait_ge(S.pm, 1)
     v.tensor_reduce(T.negM[:, :], T.psM[:, 0:N], AxisListType.X, AluOpType.max, negate=True).then_inc(S.ng, 1)
+    v.wait_ge(S.pl, 1)
+    v.tensor_scalar(T.lB[:, :], T.sel[:, :], T.psL[:, 1:2], None, mult).then_inc(S.lb, 1)
+    v.tensor_scalar(T.lC[:, :], T.sel[:, :], T.psL[:, 3:4], None, mult).then_inc(S.lc, 1)
+
     a.wait_ge(S.pm, 1)
     a.wait_ge(S.ng, 1)
-    a.activation(T.f[:, :], T.psM[:, 0:N], Ex, bias=T.negM[:, 0:1]).then_inc(S.fd, 1)
-
-    a.wait_ge(S.fd, 1)
+    a.activation(T.fb[:, 0:N], T.psM[:, 0:N], Ex, bias=T.negM[:, 0:1]).then_inc(S.fd, 1)
+    a.activation(T.f3[:, :], T.psM[:, 3:4], Ex, bias=T.negM[:, 0:1]).then_inc(S.f3d, 1)
+    a.wait_ge(S.f3d, 1)
     a.wait_ge(S.seld, 2)
-    a.activation(T.wA[0:Q, :], T.sel[0:Q, :], Cp, scale=T.f[0:Q, 0:1]).then_inc(S.wa, 1)
-    a.activation(T.wB[:, :], T.sel[:, :], Cp, scale=T.f[:, 1:2]).then_inc(S.wb, 1)
-    a.activation(T.wC[:, :], T.sel[:, :], Cp, scale=T.f[:, 3:4]).then_inc(S.wc, 1)
+    a.activation(T.wC[:, :], T.sel[:, :], Cp, scale=T.f3[:, 0:1]).then_inc(S.wc, 1)
     v.wait_ge(S.fd, 1)
-    v.wait_ge(S.pl, 1)
-    v.tensor_tensor(T.fl[:, :], T.f[:, :], T.psL[:, 0:N], AluOpType.mult).then_inc(S.fld, 1)
-    v.wait_ge(S.fld, 1)
-    v.tensor_reduce(T.den[:, :], T.fl[:, :], AxisListType.X, AluOpType.add).then_inc(S.dn, 1)
-    v.wait_ge(S.dn, 1)
-    v.reciprocal(T.rden[:, :], T.den[:, :]).then_inc(S.rd, 1)
+    v.tensor_scalar(T.wA[0:Q, :], T.sel[0:Q, :], T.fb[0:Q, 0:1], None, mult).then_inc(S.wa, 1)
+    v.tensor_scalar(T.wB[:, :], T.sel[:, :], T.fb[:, 1:2], None, mult).then_inc(S.wb, 1)
+
+    pe.wait_ge(S.fd, 1)
+    pe.wait_ge(S.la, 1)
+    pe.matmul(T.psD[0:Q, 0:1], T.lA[0:Q, :], T.fb[0:Q, 0:1], True, False).then_inc(S.dd, 1)
+    pe.wait_ge(S.lb, 1)
+    pe.matmul(T.psD[0:Q, 0:1], T.lB[:, :], T.fb[:, 1:2], False, False).then_inc(S.dd, 1)
+    pe.wait_ge(S.lc, 1)
+    pe.matmul(T.psD[0:Q, 0:1], T.lC[:, :], T.fb[:, 3:4], False, True).then_inc(S.dd, 1)
+    v.wait_ge(S.dd, 3)
+    v.reciprocal(T.rden[0:Q, :], T.psD[0:Q, 0:1]).then_inc(S.rd, 1)
 
     pe.wait_ge(S.wa, 1)
     pe.wait_ge(S.ld_a, 16)
-    pe.matmul(T.acc[0:Q, 0:D], T.wA[0:Q, :], T.oA[0:Q, :], True, False).then_inc(S.mm, 1)
-    pe.wait_ge(S.wb, 1)
-    pe.wait_ge(S.tb, 16)
-    pe.matmul(T.acc[0:Q, 0:D], T.wB[:, :], T.oB[:, :], False, False).then_inc(S.mm, 1)
+    pe.matmul(T.accL[0:Q, 0:H], T.wA[0:Q, :], T.oA[0:Q, 0:H], True, False).then_inc(S.mml, 1)
+    pe.matmul(T.accR[0:Q, 0:H], T.wA[0:Q, :], T.oA[0:Q, H:D], True, False).then_inc(S.mmr, 1)
     pe.wait_ge(S.wc, 1)
     pe.wait_ge(S.tc, 16)
-    pe.matmul(T.acc[0:Q, 0:D], T.wC[:, :], T.oC[:, :], False, True).then_inc(S.mm, 1)
+    pe.matmul(T.accL[0:Q, 0:H], T.wC[:, :], T.oC[:, 0:H], False, False).then_inc(S.mml, 1)
+    pe.matmul(T.accR[0:Q, 0:H], T.wC[:, :], T.oC[:, H:D], False, False).then_inc(S.mmr, 1)
+    pe.wait_ge(S.wb, 1)
+    pe.wait_ge(S.tb, 16)
+    pe.matmul(T.accL[0:Q, 0:H], T.wB[:, :], T.oB[:, 0:H], False, True).then_inc(S.mml, 1)
+    pe.matmul(T.accR[0:Q, 0:H], T.wB[:, :], T.oB[:, H:D], False, True).then_inc(S.mmr, 1)
 
     v.wait_ge(S.rd, 1)
-    v.wait_ge(S.mm, 3)
-    v.tensor_scalar(T.yb[0:Q, :], T.acc[0:Q, 0:D], T.rden[0:Q, 0:1], None, AluOpType.mult).then_inc(S.yd, 1)
-    sy.wait_ge(S.yd, 1)
+    v.wait_ge(S.mml, 3)
+    v.tensor_scalar(T.yb[0:Q, 0:H], T.accL[0:Q, 0:H], T.rden[0:Q, 0:1], None, mult).then_inc(S.yd, 1)
+    a.wait_ge(S.rd, 1)
+    a.wait_ge(S.mmr, 3)
+    a.activation(T.yb[0:Q, H:D], T.accR[0:Q, 0:H], Cp, scale=T.rden[0:Q, 0:1]).then_inc(S.yd, 1)
+    sy.wait_ge(S.yd, 2)
     sy.dma_start(T.y[:, :], T.yb[0:Q, :]).then_inc(S.st, 16)
     sy.wait_ge(S.st, 16)
-    g.wait_ge(S.sent, 1 + len(engines))
+    g.wait_ge(S.sent, 1 + 2 * len(engines))

from concourse.bass import DstId, RemoteDMATransfer
from concourse.mybir import AluOpType, AxisListType, ActivationFunctionType

N = 5
Q = 64
D = 128
H = D // 2

SCRATCH = {
    "oD": ("dram", [N, 128, Q], "bfloat16"),
    "mD": ("dram", [N + 1, 128, 1], "float32"),
    "oA": ("sbuf", [128, D], "bfloat16"),
    "oB": ("sbuf", [128, D], "bfloat16"),
    "oC": ("sbuf", [128, D], "bfloat16"),
    "mT": ("sbuf", [128, 256], "float32"),
    "mlS": ("sbuf", [128, 2], "float32"),
    "zb": ("sbuf", [128, Q], "bfloat16"),
    "ob": ("sbuf", [128, Q], "bfloat16"),
    "sel": ("sbuf", [128, Q], "bfloat16"),
    "of": ("sbuf", [128, 8], "float32"),
    "i5": ("sbuf", [128, 8], "float32"),
    "negM": ("sbuf", [128, 1], "float32"),
    "fb": ("sbuf", [128, 8], "bfloat16"),
    "f3": ("sbuf", [128, 1], "float32"),
    "rden": ("sbuf", [128, 1], "float32"),
    "lA": ("sbuf", [128, Q], "bfloat16"),
    "lB": ("sbuf", [128, Q], "bfloat16"),
    "lC": ("sbuf", [128, Q], "bfloat16"),
    "wA": ("sbuf", [128, Q], "bfloat16"),
    "wB": ("sbuf", [128, Q], "bfloat16"),
    "wC": ("sbuf", [128, Q], "bfloat16"),
    "yb": ("sbuf", [128, D], "bfloat16"),
    "psM": ("psum", [128, 512], "float32"),
    "psL": ("psum", [128, 512], "float32"),
    "psD": ("psum", [128, 512], "float32"),
    "accL": ("psum", [128, 512], "float32"),
    "accR": ("psum", [128, 512], "float32"),
}
SEMAPHORES = ["ld_m", "ld_m2", "ld_o", "ld_a", "ld_s", "cz", "cf", "ones", "idn5", "seld", "arr_m", "arr_ob", "arr_oc", "sent",
              "mt", "pm", "pl", "ng", "fd", "f3d", "la", "lb", "lc", "dd", "rd", "wa", "wb", "wc", "tb", "tc", "mml", "mmr",
              "yd", "st"]


def rank_program(g, core, T, topo):
    rank = T.rank_of(core)
    if rank is None:
        return
    S = T.sem
    v, a, pe, sy = g.vector, g.scalar, g.tensor, g.sync
    Ex, Cp = ActivationFunctionType.Exp, ActivationFunctionType.Copy
    mult = AluOpType.mult
    steps = list(range(1, N))
    peers = [T.cores[(rank + k) % N] for k in steps]
    slots = [N - k for k in steps]

    a.dma_start(T.mD[0], T.ml[:, :]).then_inc(S.ld_m, 16)
    sy.dma_start(T.oD[0], T.o[:, :]).then_inc(S.ld_o, 16)
    a.dma_start(T.mD[N], T.ml[:, :]).then_inc(S.ld_m2, 16)
    sy.dma_start(T.oA[0:Q, :], T.o[:, :]).then_inc(S.ld_a, 16)
    a.dma_start(T.mlS[0:Q, :], T.ml[:, :]).then_inc(S.ld_s, 16)

    v.memset(T.zb[:, :], 0.0).then_inc(S.cz, 1)
    v.memset(T.of[0:N, 0:N], 1.0).then_inc(S.cf, 1)
    a.wait_ge(S.cz, 1)
    a.activation(T.ob[:, :], T.zb[:, :], Ex).then_inc(S.ones, 1)

    allowed = topo.mask(core, peers[0])
    for d in peers:
        allowed &= topo.mask(core, d)
    engines = [e for e in range(16) if (allowed >> e) & 1]
    while 128 % len(engines):
        engines.pop()
    mask_o = 0
    for e in engines:
        mask_o |= 1 << e
    mask_m = 1 << engines[0]
    ids = []
    for d in peers:
        rid, pid = topo.addr(d, core)
        ids.append(DstId(rid=rid, pnc=pid))
    g.wait_ge(S.ld_m, 16)
    g.remote_dma_fused([RemoteDMATransfer(dst_ids=ids, dma_engine_mask=mask_m, remote_sem=S.arr_m,
                                          srcs=[T.mD[0]], dsts=[T.mD[k] for k in slots], alu_op=0)], local_sem=S.sent)
    g.wait_ge(S.ld_o, 16)
    g.remote_dma_fused([RemoteDMATransfer(dst_ids=ids[0:2], dma_engine_mask=mask_o, remote_sem=S.arr_oc,
                                          srcs=[T.oD[0]], dsts=[T.oD[k] for k in slots[0:2]], alu_op=0)], local_sem=S.sent)
    g.remote_dma_fused([RemoteDMATransfer(dst_ids=ids[2:4], dma_engine_mask=mask_o, remote_sem=S.arr_ob,
                                          srcs=[T.oD[0]], dsts=[T.oD[k] for k in slots[2:4]], alu_op=0)], local_sem=S.sent)
    got_m, got_pair = len(peers), 2 * len(engines)

    g.wait_ge(S.cf, 1)
    g.affine_select(T.i5[0:N, 0:N], T.of[0:N, 0:N], [[-1, N]], AluOpType.is_equal, 0.0, 0, 1).then_inc(S.idn5, 1)
    g.wait_ge(S.ones, 1)
    g.affine_select(T.sel[0:Q, :], T.ob[0:Q, :], [[-1, Q]], AluOpType.is_equal, 0.0, 0, 1).then_inc(S.seld, 1)
    g.affine_select(T.sel[Q:128, :], T.ob[Q:128, :], [[-1, Q]], AluOpType.is_equal, 0.0, 0, 1).then_inc(S.seld, 1)

    sy.wait_ge(S.arr_m, got_m)
    sy.wait_ge(S.ld_m, 16)
    sy.dma_start(T.mT[0:N, 0:128], T.mD[0:N]).then_inc(S.mt, 16)
    a.wait_ge(S.arr_m, got_m)
    a.wait_ge(S.ld_m2, 16)
    a.dma_start(T.mT[0:N, 128:256], T.mD[1:N + 1]).then_inc(S.mt, 16)

    sy.wait_ge(S.arr_oc, got_pair)
    sy.dma_start(T.oC[:, :], T.oD[3:5]).then_inc(S.tc, 16)
    sy.wait_ge(S.arr_ob, got_pair)
    sy.dma_start(T.oB[:, :], T.oD[1:3]).then_inc(S.tb, 16)

    pe.wait_ge(S.mt, 32)
    pe.wait_ge(S.idn5, 1)
    pe.matmul(T.psM[:, 0:N], T.mT[0:N, 0:256:2], T.i5[0:N, 0:N], True, True).then_inc(S.pm, 1)
    pe.matmul(T.psL[:, 0:N], T.mT[0:N, 1:256:2], T.i5[0:N, 0:N], True, True).then_inc(S.pl, 1)

    v.wait_ge(S.seld, 2)
    v.wait_ge(S.ld_s, 16)
    v.tensor_scalar(T.lA[0:Q, :], T.sel[0:Q, :], T.mlS[0:Q, 1:2], None, mult).then_inc(S.la, 1)
    v.wait_ge(S.pm, 1)
    v.tensor_reduce(T.negM[:, :], T.psM[:, 0:N], AxisListType.X, AluOpType.max, negate=True).then_inc(S.ng, 1)
    v.wait_ge(S.pl, 1)
    v.tensor_scalar(T.lB[:, :], T.sel[:, :], T.psL[:, 1:2], None, mult).then_inc(S.lb, 1)
    v.tensor_scalar(T.lC[:, :], T.sel[:, :], T.psL[:, 3:4], None, mult).then_inc(S.lc, 1)

    a.wait_ge(S.pm, 1)
    a.wait_ge(S.ng, 1)
    a.activation(T.fb[:, 0:N], T.psM[:, 0:N], Ex, bias=T.negM[:, 0:1]).then_inc(S.fd, 1)
    a.activation(T.f3[:, :], T.psM[:, 3:4], Ex, bias=T.negM[:, 0:1]).then_inc(S.f3d, 1)
    a.wait_ge(S.f3d, 1)
    a.wait_ge(S.seld, 2)
    a.activation(T.wC[:, :], T.sel[:, :], Cp, scale=T.f3[:, 0:1]).then_inc(S.wc, 1)
    v.wait_ge(S.fd, 1)
    v.tensor_scalar(T.wA[0:Q, :], T.sel[0:Q, :], T.fb[0:Q, 0:1], None, mult).then_inc(S.wa, 1)
    v.tensor_scalar(T.wB[:, :], T.sel[:, :], T.fb[:, 1:2], None, mult).then_inc(S.wb, 1)

    pe.wait_ge(S.fd, 1)
    pe.wait_ge(S.la, 1)
    pe.matmul(T.psD[0:Q, 0:1], T.lA[0:Q, :], T.fb[0:Q, 0:1], True, False).then_inc(S.dd, 1)
    pe.wait_ge(S.lb, 1)
    pe.matmul(T.psD[0:Q, 0:1], T.lB[:, :], T.fb[:, 1:2], False, False).then_inc(S.dd, 1)
    pe.wait_ge(S.lc, 1)
    pe.matmul(T.psD[0:Q, 0:1], T.lC[:, :], T.fb[:, 3:4], False, True).then_inc(S.dd, 1)
    v.wait_ge(S.dd, 3)
    v.reciprocal(T.rden[0:Q, :], T.psD[0:Q, 0:1]).then_inc(S.rd, 1)

    pe.wait_ge(S.wa, 1)
    pe.wait_ge(S.ld_a, 16)
    pe.matmul(T.accL[0:Q, 0:H], T.wA[0:Q, :], T.oA[0:Q, 0:H], True, False).then_inc(S.mml, 1)
    pe.matmul(T.accR[0:Q, 0:H], T.wA[0:Q, :], T.oA[0:Q, H:D], True, False).then_inc(S.mmr, 1)
    pe.wait_ge(S.wc, 1)
    pe.wait_ge(S.tc, 16)
    pe.matmul(T.accL[0:Q, 0:H], T.wC[:, :], T.oC[:, 0:H], False, False).then_inc(S.mml, 1)
    pe.matmul(T.accR[0:Q, 0:H], T.wC[:, :], T.oC[:, H:D], False, False).then_inc(S.mmr, 1)
    pe.wait_ge(S.wb, 1)
    pe.wait_ge(S.tb, 16)
    pe.matmul(T.accL[0:Q, 0:H], T.wB[:, :], T.oB[:, 0:H], False, True).then_inc(S.mml, 1)
    pe.matmul(T.accR[0:Q, 0:H], T.wB[:, :], T.oB[:, H:D], False, True).then_inc(S.mmr, 1)

    v.wait_ge(S.rd, 1)
    v.wait_ge(S.mml, 3)
    v.tensor_scalar(T.yb[0:Q, 0:H], T.accL[0:Q, 0:H], T.rden[0:Q, 0:1], None, mult).then_inc(S.yd, 1)
    a.wait_ge(S.rd, 1)
    a.wait_ge(S.mmr, 3)
    a.activation(T.yb[0:Q, H:D], T.accR[0:Q, 0:H], Cp, scale=T.rden[0:Q, 0:1]).then_inc(S.yd, 1)
    sy.wait_ge(S.yd, 2)
    sy.dma_start(T.y[:, :], T.yb[0:Q, :]).then_inc(S.st, 16)
    sy.wait_ge(S.st, 16)
    g.wait_ge(S.sent, 1 + 2 * len(engines))
